import numpy as np
import ml_dtypes


def mxq(x, axis, fmt="e4m3"):
    dtype, down = {"e4m3": (ml_dtypes.float8_e4m3fn, 7), "e5m2": (ml_dtypes.float8_e5m2, 14)}[fmt]
    v = np.moveaxis(np.asarray(x, np.float32).astype(ml_dtypes.bfloat16).astype(np.float64), axis, -1)
    blocks = v.reshape(v.shape[:-1] + (-1, 32))
    amax = np.abs(blocks).max(-1, keepdims=True)
    byte = np.maximum(np.where(amax > 0, np.frexp(amax)[1] - 1 + 127, 0) - down, 1)
    scale = np.exp2(byte - 127.0)
    codes = (blocks / scale).astype(np.float32).astype(dtype).astype(np.float64)
    return np.moveaxis((codes * scale).reshape(v.shape), -1, axis)


WIDE = False


def mx_kscale(k):
    if not WIDE:
        return np.ones(k)
    levels = np.array([10, -10, 5, -5, 0])
    if k % 512:
        return np.exp2(np.random.permutation(np.resize(levels, k // 32))).repeat(32)
    a = np.empty((k // 512, 16))
    for p in range(k // 512):
        a[p, :8] = np.random.permutation(np.resize(levels, 8))
        for g in range(8):
            far = levels[np.abs(levels - a[p, g]) >= 10]
            a[p, g + 8] = far[np.random.randint(len(far))]
    return np.exp2(a.ravel()).repeat(32)


def f64(x):
    return np.asarray(x).astype(np.float64)


def striped(idx):
    return np.tile(idx.reshape(-1, 16).T, (8, 1)).astype(np.uint16)


def unstriped(offs):
    return offs[:16].T.reshape(-1).astype(np.int64)


def pack_weight(w):
    k, n = w.shape
    w = f64(np.asarray(w, np.float32).astype(ml_dtypes.bfloat16)).reshape(k // 32, 32, n)
    amax = np.abs(w).max(1)
    byte = np.clip(np.where(amax > 0, np.frexp(amax)[1] - 1 + 127 - 7, 1), 1, 254)
    scaled = (w * np.exp2(127.0 - byte)[:, None, :]).reshape(k, n).astype(np.float32)
    words = np.ascontiguousarray(scaled.reshape(k // 512, 128, 4, n).transpose(0, 1, 3, 2)).astype(ml_dtypes.float8_e4m3fn).view(np.uint8)
    return words, np.ascontiguousarray(byte.astype(np.uint8).reshape(k // 512, 16, n))


def unpack_weight(words, scales):
    g, p, n, _ = words.shape
    vals = np.ascontiguousarray(words).view(ml_dtypes.float8_e4m3fn).astype(np.float64) * np.repeat(np.exp2(scales.astype(np.float64) - 127.0), 8, axis=1)[..., None]
    return vals.transpose(0, 1, 3, 2).reshape(g * 512, n)


K, T, S, V, R = 512, 1024, 512, 512, 256


def setup_inputs():
    n = np.random.standard_normal
    s = mx_kscale(K)[:, None]
    packed_xT = pack_weight(n((K, T)) * s)
    return {
        "x_words": packed_xT[0],
        "x_scales": packed_xT[1],
        "hT": (n((K, V)) / np.sqrt(K) / s).astype(np.float32),
        "att": (np.random.uniform(0.0, 1.0, (V, R)) ** 4 / R * 5).astype(np.float32),
        "cpw": (np.random.uniform(0.2, 0.8, (V, 1))).astype(np.float32),
        "gen": (np.random.uniform(0.2, 0.8, (V, 1))).astype(np.float32),
        "offs": striped(np.random.permutation(T)[:S]),
        "src": striped(np.random.permutation(S)[:R]),
    }


def reference(x_words, x_scales, hT, att, cpw, gen, offs, src):
    hTq = mxq(f64(hT), 0, "e4m3")
    xq = unpack_weight(x_words, x_scales)[:, unstriped(offs)]
    y = hTq.T @ xq
    ex = np.exp(y - y.max(axis=1, keepdims=True))
    p = ex / ex.sum(axis=1, keepdims=True)
    cp = np.zeros((K, S))
    cp[:, unstriped(src)] = f64(cpw) * f64(att)
    return np.log(f64(gen) * p + cp + 1e-3)

@@ -1,0 +1,139 @@
+from contextlib import ExitStack
+
+import concourse.mybir as mybir
+
+K, T, S, V, R = 512, 1024, 512, 512, 256
+FLOPS = 2 * K * V * S
+
+F32 = mybir.dt.float32
+BF16 = mybir.dt.bfloat16
+I32 = mybir.dt.int32
+U32 = mybir.dt.uint32
+U16 = mybir.dt.uint16
+U8 = mybir.dt.uint8
+FP8X4 = mybir.dt.float8_e4m3fn_x4
+ACT = mybir.ActivationFunctionType
+ALU = mybir.AluOpType
+
+P = 128
+PACK = 4
+HALF = V // 2
+EPS = 1e-3
+
+
+def tile_picked_ycopy_log_p_kernel(tc, x_words, x_scales, hT, att, cpw, gen, offs, src, out):
+    nc = tc.nc
+    with ExitStack() as ctx:
+        keep = ctx.enter_context(tc.tile_pool(name="keep", bufs=1))
+        psum = ctx.enter_context(tc.psum_pool(name="psum", bufs=1))
+
+        offs_sb = keep.tile([P, S // 16], U16, name="offs_sb")
+        src_sb = keep.tile([P, R // 16], U16, name="src_sb")
+        words = keep.tile([P, T], I32, name="words")
+        scale_bytes = keep.tile([P, T], U8, name="scale_bytes")
+        h_raw = [keep.tile([P, PACK, HALF], F32, name="h_raw%d" % h) for h in range(2)]
+        att_sb = [keep.tile([P, R], F32, name="att_sb%d" % i) for i in range(2)]
+        att_late = keep.tile([P, 2, R], F32, name="att_late")
+        cpw_sb = keep.tile([P, 2, 2], F32, name="cpw_sb")
+        gen_sb = keep.tile([P, 2, 2], F32, name="gen_sb")
+
+        h_rows = hT.rearrange("(p j) t -> p j t", j=PACK)
+        att_rows = att.rearrange("(h p c) r -> h p c r", h=2, c=2)
+        out_rows = out.rearrange("(h p c) j -> h p c j", h=2, c=2)
+
+        nc.vector.memset(scale_bytes[:].bitcast(I32), 0)
+        for q in range(4):
+            nc.scalar.dma_start(out=scale_bytes[32 * q : 32 * q + 4, :].bitcast(I32), in_=x_scales[0, 4 * q : 4 * q + 4, :].bitcast(I32))
+        nc.sync.dma_start(offs_sb[:], offs)
+        nc.sync.dma_start(src_sb[:], src)
+        nc.sync.dma_start(out=words[:], in_=x_words[0].rearrange("p n t -> p (n t)").bitcast(I32))
+        nc.sync.dma_start(out=att_sb[0][:], in_=att_rows[0, :, 0, :])
+        nc.sync.dma_start(out=cpw_sb[:], in_=cpw.rearrange("(h p c) o -> p h (c o)", h=2, c=2))
+        nc.sync.dma_start(out=h_raw[0][:], in_=h_rows[:, :, 0:HALF])
+        nc.sync.dma_start(out=att_sb[1][:], in_=att_rows[0, :, 1, :])
+        nc.sync.dma_start(out=h_raw[1][:], in_=h_rows[:, :, HALF:V])
+        nc.sync.dma_start(out=gen_sb[:], in_=gen.rearrange("(h p c) o -> p h (c o)", h=2, c=2))
+        nc.sync.dma_start(out=att_late[:], in_=att_rows[1])
+
+        windows = [keep.tile([P, S], F32, name="window%d" % c) for c in range(2)]
+        for c in range(2):
+            nc.vector.memset(windows[c][:], 0.0)
+
+        x_codes = keep.tile([P, S], U32, name="x_codes", align_bytes=64)
+        x_plane = keep.tile([P, S], U8, name="x_plane", align_bytes=64)
+        nc.vector.tensor_copy(x_plane[:], scale_bytes[:].indirect(offs_sb[:]))
+        nc.vector.tensor_copy(x_codes[:], words[:].bitcast(U32).indirect(offs_sb[:]))
+
+        neg_max = h_raw[1][:, 0, 0:4]
+        sums = keep.tile([P, 4], F32, name="sums")
+        inv = keep.tile([P, 4], F32, name="inv")
+        factor = keep.tile([P, 4], F32, name="factor")
+        copied = [keep.tile([P, R], F32, name="copied%d" % i)[:] if i != 1 else h_raw[0][:, 0, :] for i in range(4)]
+        expd = [keep.tile([P, S], F32, name="expd%d" % i) for i in range(4)]
+        mixed = [keep.tile([P, S], F32, name="mixed%d" % i) for i in range(4)]
+        logs = [keep.tile([P, S], F32, name="logs%d" % i) for i in range(4)]
+        banks = [psum.tile([P, S], F32, name="bank%d" % i) for i in range(4)]
+
+        def weigh(i):
+            rows = att_sb[i][:] if i < 2 else att_late[:, i - 2, :]
+            nc.scalar.activation(copied[i], rows, ACT.Copy, scale=cpw_sb[:, i // 2, i % 2 : i % 2 + 1])
+
+        def scatter(i):
+            nc.vector.tensor_copy(windows[i % 2][:].indirect(src_sb[:]), copied[i])
+
+        def product(h):
+            grouped = keep.tile([P, 2, P, PACK], BF16, name="grouped%d" % h, align_bytes=64)
+            nc.scalar.copy(
+                grouped[:].rearrange("p c (a b) j -> p a j b c", b=2),
+                h_raw[h][:].rearrange("p j (a b c) -> p a j b c", b=2, c=2),
+            )
+            h_codes = keep.tile([P, HALF], U32, name="h_codes%d" % h, align_bytes=64)
+            h_plane = keep.tile([P, HALF], U8, name="h_plane%d" % h, align_bytes=64)
+            nc.vector.quantize_mx(out=h_codes[:].bitcast(FP8X4), scales=h_plane[:], in_=grouped[:].rearrange("p c m j -> p (c m j)"))
+            for c in range(2):
+                cols = slice(c * P, (c + 1) * P)
+                nc.tensor.matmul_mx(
+                    out=banks[2 * h + c][:],
+                    lhsT=h_codes[:, cols].bitcast(FP8X4),
+                    lhsT_scale=h_plane[:, cols],
+                    rhs=x_codes[:].bitcast(FP8X4),
+                    rhs_scale=x_plane[:],
+                    start=True,
+                    stop=True,
+                )
+
+        def exponentiate(i):
+            col = slice(i, i + 1)
+            nc.vector.tensor_reduce(neg_max[:, col], banks[i][:], mybir.AxisListType.X, ALU.max, negate=True)
+            nc.scalar.activation(expd[i][:], banks[i][:], ACT.Exp, bias=neg_max[:, col], accum_out=sums[:, col])
+
+        def normalise(h):
+            cols = slice(2 * h, 2 * h + 2)
+            nc.vector.reciprocal(inv[:, cols], sums[:, cols])
+            nc.vector.tensor_tensor(factor[:, cols], inv[:, cols], gen_sb[:, h, :], ALU.mult)
+
+        def finish(i, cols):
+            nc.vector.scalar_tensor_tensor(mixed[i][:, cols], expd[i][:, cols], factor[:, i : i + 1], windows[i % 2][:, cols], ALU.mult, ALU.add)
+            nc.scalar.activation(logs[i][:, cols], mixed[i][:, cols], ACT.Ln, bias=EPS)
+            nc.sync.dma_start(out=out_rows[i // 2, :, i % 2, cols], in_=logs[i][:, cols])
+
+        weigh(0)
+        scatter(0)
+        product(0)
+        weigh(1)
+        scatter(1)
+        product(1)
+        for i in range(4):
+            exponentiate(i)
+        for h in range(2):
+            normalise(h)
+        whole = slice(0, S)
+        weigh(2)
+        weigh(3)
+        finish(0, whole)
+        scatter(2)
+        finish(1, whole)
+        finish(2, whole)
+        scatter(3)
+        finish(3, slice(0, S // 2))
+        finish(3, slice(S // 2, S))

@@ -32,57 +32,65 @@ def tile_picked_ycopy_log_p_kernel(tc, x_words, x_scales, hT, att, cpw, gen, off
         words = keep.tile([P, T], I32, name="words")
         scale_bytes = keep.tile([P, T], U8, name="scale_bytes")
         h_raw = [keep.tile([P, PACK, HALF], F32, name="h_raw%d" % h) for h in range(2)]
-        att_sb = [keep.tile([P, R], F32, name="att_sb%d" % i) for i in range(2)]
+        att_first = keep.tile([P, R], F32, name="att_first")
+        att_second = keep.tile([P, R], F32, name="att_second")
         att_late = keep.tile([P, 2, R], F32, name="att_late")
-        cpw_sb = keep.tile([P, 2, 2], F32, name="cpw_sb")
-        gen_sb = keep.tile([P, 2, 2], F32, name="gen_sb")
+        att_sb = [att_first[:], att_second[:], att_late[:, 0, :], att_late[:, 1, :]]
+        cpw_sb = keep.tile([P, 2, 8], F32, name="cpw_sb")
+        gen_sb = keep.tile([P, 2, 8], F32, name="gen_sb")
 
         h_rows = hT.rearrange("(p j) t -> p j t", j=PACK)
         att_rows = att.rearrange("(h p c) r -> h p c r", h=2, c=2)
         out_rows = out.rearrange("(h p c) j -> h p c j", h=2, c=2)
 
         nc.vector.memset(scale_bytes[:].bitcast(I32), 0)
-        for q in range(4):
-            nc.scalar.dma_start(out=scale_bytes[32 * q : 32 * q + 4, :].bitcast(I32), in_=x_scales[0, 4 * q : 4 * q + 4, :].bitcast(I32))
-        nc.sync.dma_start(offs_sb[:], offs)
         nc.sync.dma_start(src_sb[:], src)
+        nc.sync.dma_start(out=cpw_sb[:, :, 0:2], in_=cpw.rearrange("(h p c) o -> p h (c o)", h=2, c=2))
+        nc.sync.dma_start(out=att_first[:], in_=att_rows[0, :, 0, :])
+        nc.sync.dma_start(offs_sb[:], offs)
         nc.sync.dma_start(out=words[:], in_=x_words[0].rearrange("p n t -> p (n t)").bitcast(I32))
-        nc.sync.dma_start(out=att_sb[0][:], in_=att_rows[0, :, 0, :])
-        nc.sync.dma_start(out=cpw_sb[:], in_=cpw.rearrange("(h p c) o -> p h (c o)", h=2, c=2))
         nc.sync.dma_start(out=h_raw[0][:], in_=h_rows[:, :, 0:HALF])
-        nc.sync.dma_start(out=att_sb[1][:], in_=att_rows[0, :, 1, :])
+        for q in range(4):
+            nc.sync.dma_start(out=scale_bytes[32 * q : 32 * q + 4, :].bitcast(I32), in_=x_scales[0, 4 * q : 4 * q + 4, :].bitcast(I32))
         nc.sync.dma_start(out=h_raw[1][:], in_=h_rows[:, :, HALF:V])
-        nc.sync.dma_start(out=gen_sb[:], in_=gen.rearrange("(h p c) o -> p h (c o)", h=2, c=2))
+        nc.sync.dma_start(out=att_second[:], in_=att_rows[0, :, 1, :])
         nc.sync.dma_start(out=att_late[:], in_=att_rows[1])
+        nc.sync.dma_start(out=gen_sb[:, :, 0:2], in_=gen.rearrange("(h p c) o -> p h (c o)", h=2, c=2))
 
-        windows = [keep.tile([P, S], F32, name="window%d" % c) for c in range(2)]
-        for c in range(2):
-            nc.vector.memset(windows[c][:], 0.0)
+        windows = [keep.tile([P, S], F32, name="window%d" % c) for c in range(3)]
+        nc.vector.memset(windows[0][:], 0.0)
+        nc.vector.memset(windows[2][:], 0.0)
+        nc.scalar.activation(windows[1][:], windows[2][:], ACT.Copy)
 
-        x_codes = keep.tile([P, S], U32, name="x_codes", align_bytes=64)
-        x_plane = keep.tile([P, S], U8, name="x_plane", align_bytes=64)
-        nc.vector.tensor_copy(x_plane[:], scale_bytes[:].indirect(offs_sb[:]))
-        nc.vector.tensor_copy(x_codes[:], words[:].bitcast(U32).indirect(offs_sb[:]))
-
-        neg_max = h_raw[1][:, 0, 0:4]
         sums = keep.tile([P, 4], F32, name="sums")
         inv = keep.tile([P, 4], F32, name="inv")
-        factor = keep.tile([P, 4], F32, name="factor")
-        copied = [keep.tile([P, R], F32, name="copied%d" % i)[:] if i != 1 else h_raw[0][:, 0, :] for i in range(4)]
+        factor = keep.tile([P, 2], F32, name="factor")
+        table_warm = keep.tile([P, 1], F32, name="table_warm")
         expd = [keep.tile([P, S], F32, name="expd%d" % i) for i in range(4)]
-        mixed = [keep.tile([P, S], F32, name="mixed%d" % i) for i in range(4)]
+        mixed = {i: keep.tile([P, S], F32, name="mixed%d" % i) for i in (0, 1, 3)}
         logs = [keep.tile([P, S], F32, name="logs%d" % i) for i in range(4)]
         banks = [psum.tile([P, S], F32, name="bank%d" % i) for i in range(4)]
 
-        def weigh(i):
-            rows = att_sb[i][:] if i < 2 else att_late[:, i - 2, :]
-            nc.scalar.activation(copied[i], rows, ACT.Copy, scale=cpw_sb[:, i // 2, i % 2 : i % 2 + 1])
+        def column(vec, i):
+            return vec[:, i // 2, i % 2 : i % 2 + 1]
 
-        def scatter(i):
-            nc.vector.tensor_copy(windows[i % 2][:].indirect(src_sb[:]), copied[i])
+        def weigh(i, copied, lo=0, hi=R):
+            nc.scalar.activation(copied, att_sb[i][:, lo:hi], ACT.Copy, scale=column(cpw_sb, i))
 
-        def product(h):
-            grouped = keep.tile([P, 2, P, PACK], BF16, name="grouped%d" % h, align_bytes=64)
+        def scatter(i, copied, lo=0, hi=R):
+            nc.vector.tensor_copy(windows[i % 3][:].indirect(src_sb[:, lo // 16 : hi // 16]), copied)
+
+        copied_first = keep.tile([P, R], F32, name="copied_first")
+        weigh(0, copied_first[:])
+        scatter(0, copied_first[:])
+
+        x_codes = keep.tile([P, S], U32, name="x_codes", align_bytes=64)
+        x_plane = keep.tile([P, S], U8, name="x_plane", align_bytes=64)
+        nc.vector.tensor_copy(x_codes[:], words[:].bitcast(U32).indirect(offs_sb[:]))
+        nc.vector.tensor_copy(x_plane[:], scale_bytes[:].indirect(offs_sb[:]))
+
+        for h in range(2):
+            grouped = keep.tile([P, 2, P, PACK], BF16, name="grouped%d" % h, tag="grouped%d" % h, align_bytes=64)
             nc.scalar.copy(
                 grouped[:].rearrange("p c (a b) j -> p a j b c", b=2),
                 h_raw[h][:].rearrange("p j (a b c) -> p a j b c", b=2, c=2),
@@ -102,38 +110,52 @@ def tile_picked_ycopy_log_p_kernel(tc, x_words, x_scales, hT, att, cpw, gen, off
                     stop=True,
                 )
 
+        copied_early = keep.tile([P, R // 2], F32, name="copied_early")
+        weigh(1, copied_early[:], 0, R // 2)
+        scatter(1, copied_early[:], 0, R // 2)
+
+        late = keep.tile([P, 4, R], F32, name="late", tag="grouped1", align_bytes=64)
+        neg_max = [late[:, 0, i : i + 1] for i in range(4)]
+        scaled = keep.tile([P, S], F32, name="scaled")
+
         def exponentiate(i):
             col = slice(i, i + 1)
-            nc.vector.tensor_reduce(neg_max[:, col], banks[i][:], mybir.AxisListType.X, ALU.max, negate=True)
-            nc.scalar.activation(expd[i][:], banks[i][:], ACT.Exp, bias=neg_max[:, col], accum_out=sums[:, col])
+            nc.vector.tensor_reduce(neg_max[i], banks[i][:], mybir.AxisListType.X, ALU.max, negate=True)
+            nc.scalar.activation(expd[i][:], banks[i][:], ACT.Exp, bias=neg_max[i], accum_out=sums[:, col])
 
-        def normalise(h):
-            cols = slice(2 * h, 2 * h + 2)
-            nc.vector.reciprocal(inv[:, cols], sums[:, cols])
-            nc.vector.tensor_tensor(factor[:, cols], inv[:, cols], gen_sb[:, h, :], ALU.mult)
+        def mix_on_gpsimd(i):
+            nc.gpsimd.tensor_scalar(scaled[:], expd[i][:], inv[:, i : i + 1], column(gen_sb, i), ALU.mult, ALU.mult)
+            nc.gpsimd.tensor_tensor(mixed[i][:], scaled[:], windows[i][:], ALU.add)
 
-        def finish(i, cols):
-            nc.vector.scalar_tensor_tensor(mixed[i][:, cols], expd[i][:, cols], factor[:, i : i + 1], windows[i % 2][:, cols], ALU.mult, ALU.add)
-            nc.scalar.activation(logs[i][:, cols], mixed[i][:, cols], ACT.Ln, bias=EPS)
+        def mix_on_vector(i, cols, target):
+            nc.vector.scalar_tensor_tensor(target, expd[i][:, cols], factor[:, i - 2 : i - 1], windows[i % 3][:, cols], ALU.mult, ALU.add)
+
+        def finish(i, cols, source):
+            nc.scalar.activation(logs[i][:, cols], source, ACT.Ln, bias=EPS)
             nc.sync.dma_start(out=out_rows[i // 2, :, i % 2, cols], in_=logs[i][:, cols])
 
-        weigh(0)
-        scatter(0)
-        product(0)
-        weigh(1)
-        scatter(1)
-        product(1)
         for i in range(4):
             exponentiate(i)
-        for h in range(2):
-            normalise(h)
+            if i < 2:
+                nc.vector.reciprocal(inv[:, i : i + 1], sums[:, i : i + 1])
+        nc.vector.reciprocal(inv[:, 2:4], sums[:, 2:4])
+        nc.scalar.activation(table_warm[:], sums[:, 3:4], ACT.Ln)
+        for i in range(2, 4):
+            nc.scalar.activation(factor[:, i - 2 : i - 1], inv[:, i : i + 1], ACT.Copy, scale=column(gen_sb, i))
+        weigh(1, late[:, 1, 0 : R // 2], R // 2, R)
+        weigh(2, late[:, 2, :])
+        weigh(3, late[:, 3, :])
         whole = slice(0, S)
-        weigh(2)
-        weigh(3)
-        finish(0, whole)
-        scatter(2)
-        finish(1, whole)
-        finish(2, whole)
-        scatter(3)
-        finish(3, slice(0, S // 2))
-        finish(3, slice(S // 2, S))
+        mix_on_gpsimd(0)
+        scatter(1, late[:, 1, 0 : R // 2], R // 2, R)
+        mix_on_gpsimd(1)
+        scatter(2, late[:, 2, :])
+        scatter(3, late[:, 3, :])
+        for i in range(2):
+            finish(i, whole, mixed[i][:])
+        reused = late[:, 2:4, :].rearrange("p a r -> p (a r)")
+        mix_on_vector(2, whole, reused)
+        finish(2, whole, reused)
+        for cols in (slice(0, S // 2), slice(S // 2, S)):
+            mix_on_vector(3, cols, mixed[3][:, cols])
+            finish(3, cols, mixed[3][:, cols])

from contextlib import ExitStack

import concourse.mybir as mybir

K, T, S, V, R = 512, 1024, 512, 512, 256
FLOPS = 2 * K * V * S

F32 = mybir.dt.float32
BF16 = mybir.dt.bfloat16
I32 = mybir.dt.int32
U32 = mybir.dt.uint32
U16 = mybir.dt.uint16
U8 = mybir.dt.uint8
FP8X4 = mybir.dt.float8_e4m3fn_x4
ACT = mybir.ActivationFunctionType
ALU = mybir.AluOpType

P = 128
PACK = 4
HALF = V // 2
EPS = 1e-3


def tile_picked_ycopy_log_p_kernel(tc, x_words, x_scales, hT, att, cpw, gen, offs, src, out):
    nc = tc.nc
    with ExitStack() as ctx:
        keep = ctx.enter_context(tc.tile_pool(name="keep", bufs=1))
        psum = ctx.enter_context(tc.psum_pool(name="psum", bufs=1))

        offs_sb = keep.tile([P, S // 16], U16, name="offs_sb")
        src_sb = keep.tile([P, R // 16], U16, name="src_sb")
        words = keep.tile([P, T], I32, name="words")
        scale_bytes = keep.tile([P, T], U8, name="scale_bytes")
        h_raw = [keep.tile([P, PACK, HALF], F32, name="h_raw%d" % h) for h in range(2)]
        att_first = keep.tile([P, R], F32, name="att_first")
        att_second = keep.tile([P, R], F32, name="att_second")
        att_late = keep.tile([P, 2, R], F32, name="att_late")
        att_sb = [att_first[:], att_second[:], att_late[:, 0, :], att_late[:, 1, :]]
        cpw_sb = keep.tile([P, 2, 8], F32, name="cpw_sb")
        gen_sb = keep.tile([P, 2, 8], F32, name="gen_sb")

        h_rows = hT.rearrange("(p j) t -> p j t", j=PACK)
        att_rows = att.rearrange("(h p c) r -> h p c r", h=2, c=2)
        out_rows = out.rearrange("(h p c) j -> h p c j", h=2, c=2)

        nc.vector.memset(scale_bytes[:].bitcast(I32), 0)
        nc.sync.dma_start(src_sb[:], src)
        nc.sync.dma_start(out=cpw_sb[:, :, 0:2], in_=cpw.rearrange("(h p c) o -> p h (c o)", h=2, c=2))
        nc.sync.dma_start(out=att_first[:], in_=att_rows[0, :, 0, :])
        nc.sync.dma_start(offs_sb[:], offs)
        nc.sync.dma_start(out=words[:], in_=x_words[0].rearrange("p n t -> p (n t)").bitcast(I32))
        nc.sync.dma_start(out=h_raw[0][:], in_=h_rows[:, :, 0:HALF])
        for q in range(4):
            nc.sync.dma_start(out=scale_bytes[32 * q : 32 * q + 4, :].bitcast(I32), in_=x_scales[0, 4 * q : 4 * q + 4, :].bitcast(I32))
        nc.sync.dma_start(out=h_raw[1][:], in_=h_rows[:, :, HALF:V])
        nc.sync.dma_start(out=att_second[:], in_=att_rows[0, :, 1, :])
        nc.sync.dma_start(out=att_late[:], in_=att_rows[1])
        nc.sync.dma_start(out=gen_sb[:, :, 0:2], in_=gen.rearrange("(h p c) o -> p h (c o)", h=2, c=2))

        windows = [keep.tile([P, S], F32, name="window%d" % c) for c in range(3)]
        nc.vector.memset(windows[0][:], 0.0)
        nc.vector.memset(windows[2][:], 0.0)
        nc.scalar.activation(windows[1][:], windows[2][:], ACT.Copy)

        sums = keep.tile([P, 4], F32, name="sums")
        inv = keep.tile([P, 4], F32, name="inv")
        factor = keep.tile([P, 2], F32, name="factor")
        table_warm = keep.tile([P, 1], F32, name="table_warm")
        expd = [keep.tile([P, S], F32, name="expd%d" % i) for i in range(4)]
        mixed = {i: keep.tile([P, S], F32, name="mixed%d" % i) for i in (0, 1, 3)}
        logs = [keep.tile([P, S], F32, name="logs%d" % i) for i in range(4)]
        banks = [psum.tile([P, S], F32, name="bank%d" % i) for i in range(4)]

        def column(vec, i):
            return vec[:, i // 2, i % 2 : i % 2 + 1]

        def weigh(i, copied, lo=0, hi=R):
            nc.scalar.activation(copied, att_sb[i][:, lo:hi], ACT.Copy, scale=column(cpw_sb, i))

        def scatter(i, copied, lo=0, hi=R):
            nc.vector.tensor_copy(windows[i % 3][:].indirect(src_sb[:, lo // 16 : hi // 16]), copied)

        copied_first = keep.tile([P, R], F32, name="copied_first")
        weigh(0, copied_first[:])
        scatter(0, copied_first[:])

        x_codes = keep.tile([P, S], U32, name="x_codes", align_bytes=64)
        x_plane = keep.tile([P, S], U8, name="x_plane", align_bytes=64)
        nc.vector.tensor_copy(x_codes[:], words[:].bitcast(U32).indirect(offs_sb[:]))
        nc.vector.tensor_copy(x_plane[:], scale_bytes[:].indirect(offs_sb[:]))

        for h in range(2):
            grouped = keep.tile([P, 2, P, PACK], BF16, name="grouped%d" % h, tag="grouped%d" % h, align_bytes=64)
            nc.scalar.copy(
                grouped[:].rearrange("p c (a b) j -> p a j b c", b=2),
                h_raw[h][:].rearrange("p j (a b c) -> p a j b c", b=2, c=2),
            )
            h_codes = keep.tile([P, HALF], U32, name="h_codes%d" % h, align_bytes=64)
            h_plane = keep.tile([P, HALF], U8, name="h_plane%d" % h, align_bytes=64)
            nc.vector.quantize_mx(out=h_codes[:].bitcast(FP8X4), scales=h_plane[:], in_=grouped[:].rearrange("p c m j -> p (c m j)"))
            for c in range(2):
                cols = slice(c * P, (c + 1) * P)
                nc.tensor.matmul_mx(
                    out=banks[2 * h + c][:],
                    lhsT=h_codes[:, cols].bitcast(FP8X4),
                    lhsT_scale=h_plane[:, cols],
                    rhs=x_codes[:].bitcast(FP8X4),
                    rhs_scale=x_plane[:],
                    start=True,
                    stop=True,
                )

        copied_early = keep.tile([P, R // 2], F32, name="copied_early")
        weigh(1, copied_early[:], 0, R // 2)
        scatter(1, copied_early[:], 0, R // 2)

        late = keep.tile([P, 4, R], F32, name="late", tag="grouped1", align_bytes=64)
        neg_max = [late[:, 0, i : i + 1] for i in range(4)]
        scaled = keep.tile([P, S], F32, name="scaled")

        def exponentiate(i):
            col = slice(i, i + 1)
            nc.vector.tensor_reduce(neg_max[i], banks[i][:], mybir.AxisListType.X, ALU.max, negate=True)
            nc.scalar.activation(expd[i][:], banks[i][:], ACT.Exp, bias=neg_max[i], accum_out=sums[:, col])

        def mix_on_gpsimd(i):
            nc.gpsimd.tensor_scalar(scaled[:], expd[i][:], inv[:, i : i + 1], column(gen_sb, i), ALU.mult, ALU.mult)
            nc.gpsimd.tensor_tensor(mixed[i][:], scaled[:], windows[i][:], ALU.add)

        def mix_on_vector(i, cols, target):
            nc.vector.scalar_tensor_tensor(target, expd[i][:, cols], factor[:, i - 2 : i - 1], windows[i % 3][:, cols], ALU.mult, ALU.add)

        def finish(i, cols, source):
            nc.scalar.activation(logs[i][:, cols], source, ACT.Ln, bias=EPS)
            nc.sync.dma_start(out=out_rows[i // 2, :, i % 2, cols], in_=logs[i][:, cols])

        for i in range(4):
            exponentiate(i)
            if i < 2:
                nc.vector.reciprocal(inv[:, i : i + 1], sums[:, i : i + 1])
        nc.vector.reciprocal(inv[:, 2:4], sums[:, 2:4])
        nc.scalar.activation(table_warm[:], sums[:, 3:4], ACT.Ln)
        for i in range(2, 4):
            nc.scalar.activation(factor[:, i - 2 : i - 1], inv[:, i : i + 1], ACT.Copy, scale=column(gen_sb, i))
        weigh(1, late[:, 1, 0 : R // 2], R // 2, R)
        weigh(2, late[:, 2, :])
        weigh(3, late[:, 3, :])
        whole = slice(0, S)
        mix_on_gpsimd(0)
        scatter(1, late[:, 1, 0 : R // 2], R // 2, R)
        mix_on_gpsimd(1)
        scatter(2, late[:, 2, :])
        scatter(3, late[:, 3, :])
        for i in range(2):
            finish(i, whole, mixed[i][:])
        reused = late[:, 2:4, :].rearrange("p a r -> p (a r)")
        mix_on_vector(2, whole, reused)
        finish(2, whole, reused)
        for cols in (slice(0, S // 2), slice(S // 2, S)):
            mix_on_vector(3, cols, mixed[3][:, cols])
            finish(3, cols, mixed[3][:, cols])
